import numpy as np
import ml_dtypes


def mxq(x, axis, fmt="e4m3"):
    dtype, down = {"e4m3": (ml_dtypes.float8_e4m3fn, 7), "e5m2": (ml_dtypes.float8_e5m2, 14)}[fmt]
    v = np.moveaxis(np.asarray(x, np.float32).astype(ml_dtypes.bfloat16).astype(np.float64), axis, -1)
    blocks = v.reshape(v.shape[:-1] + (-1, 32))
    amax = np.abs(blocks).max(-1, keepdims=True)
    byte = np.maximum(np.where(amax > 0, np.frexp(amax)[1] - 1 + 127, 0) - down, 1)
    scale = np.exp2(byte - 127.0)
    codes = (blocks / scale).astype(np.float32).astype(dtype).astype(np.float64)
    return np.moveaxis((codes * scale).reshape(v.shape), -1, axis)


WIDE = False


def mx_kscale(k):
    if not WIDE:
        return np.ones(k)
    levels = np.array([10, -10, 5, -5, 0])
    if k % 512:
        return np.exp2(np.random.permutation(np.resize(levels, k // 32))).repeat(32)
    a = np.empty((k // 512, 16))
    for p in range(k // 512):
        a[p, :8] = np.random.permutation(np.resize(levels, 8))
        for g in range(8):
            far = levels[np.abs(levels - a[p, g]) >= 10]
            a[p, g + 8] = far[np.random.randint(len(far))]
    return np.exp2(a.ravel()).repeat(32)


BF16 = ml_dtypes.bfloat16


def bf(x):
    return np.asarray(x, np.float32).astype(BF16)


def f64(x):
    return np.asarray(x).astype(np.float64)


E2M1 = np.array([0.0, 0.5, 1.0, 1.5, 2.0, 3.0, 4.0, 6.0, -0.0, -0.5, -1.0, -1.5, -2.0, -3.0, -4.0, -6.0])


def pack_weight(w, fmt):
    k, n = w.shape
    w = f64(bf(w)).reshape(k // 32, 32, n)
    amax = np.abs(w).max(1)
    if fmt == "e4m3":
        byte = np.frexp(amax)[1] - 1 + 127 - 7
    else:
        mant, ex = np.frexp(amax / 6.0)
        byte = np.where(mant > 0.5, ex, ex - 1) + 127
    byte = np.clip(np.where(amax > 0, byte, 1), 1, 254)
    scaled = (w * np.exp2(127.0 - byte)[:, None, :]).reshape(k, n).astype(np.float32)
    by_word = np.ascontiguousarray(scaled.reshape(k // 512, 128, 4, n).transpose(0, 1, 3, 2))
    if fmt == "e4m3":
        words = by_word.astype(ml_dtypes.float8_e4m3fn).view(np.uint8)
    else:
        c = by_word.astype(ml_dtypes.float4_e2m1fn).view(np.uint8) & 0xF
        words = c[..., 0::2] | (c[..., 1::2] << 4)
    return np.ascontiguousarray(words), np.ascontiguousarray(byte.astype(np.uint8).reshape(k // 512, 16, n))


def unpack_weight(words, scales, fmt):
    g, p, n, _ = words.shape
    if fmt == "e4m3":
        vals = np.ascontiguousarray(words).view(ml_dtypes.float8_e4m3fn).astype(np.float64)
    else:
        nib = np.empty((g, p, n, 4), np.uint8)
        nib[..., 0::2] = words & 0xF
        nib[..., 1::2] = words >> 4
        vals = E2M1[nib]
    vals = vals * np.repeat(np.exp2(scales.astype(np.float64) - 127.0), 8, axis=1)[..., None]
    return vals.transpose(0, 1, 3, 2).reshape(g * 512, n)
def pack4(w):
    words, scales = pack_weight(w, "e2m1")
    return words.reshape(words.shape[0], 128, -1), scales


def unpack4(words, scales):
    return unpack_weight(words.reshape(words.shape[0], 128, -1, 2), scales, "e2m1")


def planes(Y):
    n, m = Y.shape
    b = f64(bf(Y)).reshape(n // 32, 32, m)
    amax = np.abs(b).max(1)
    byte = np.clip(np.where(amax > 0, np.frexp(amax)[1] - 1 + 127 - 7, 1), 1, 254)
    codes = (b * np.exp2(127.0 - byte)[:, None, :]).reshape(n, m).astype(np.float32).astype(ml_dtypes.float8_e4m3fn).view(np.uint8)
    words = codes.reshape(n // 512, 128, 4, m).transpose(0, 1, 3, 2)
    return np.ascontiguousarray(words), np.ascontiguousarray(byte.astype(np.uint8).reshape(n // 512, 16, m))


M, T, F, N = 1024, 1024, 1536, 2048

def setup_inputs():
    s = mx_kscale(T)
    t = mx_kscale(F)
    x = np.random.randn(T, M) * s[:, None]
    x_words, x_scales = pack_weight(x, "e4m3")
    w = np.random.randn(T, F) / np.sqrt(T) / s[:, None] * t[None, :]
    w_words, w_scales = pack4(w)
    base = (0.3 + 0.3 * np.random.randn(F)) * t
    level = np.exp(0.6 * np.random.randn(N))
    r = np.exp(2.0 * np.random.randn(F, N))
    r = 2.0 * level[None, :] * r / r.sum(axis=0, keepdims=True)
    recipe = r / t[:, None]
    safety = level * (0.3 + 0.1 * np.random.randn(N))
    lot = level * np.abs(1.2 + 0.3 * np.random.randn(N))
    share = 1.0 / (1.0 + np.exp(-np.random.randn(N)))
    return {"x_words": x_words, "x_scales": x_scales, "w_words": w_words, "w_scales": w_scales,
            "base": bf(base), "recipe": bf(recipe), "safety": bf(safety), "lot": bf(lot), "share": bf(share)}

def reference(x_words, x_scales, w_words, w_scales, base, recipe, safety, lot, share):
    X = unpack_weight(x_words, x_scales, "e4m3")
    W = unpack4(w_words, w_scales)
    H = np.maximum((X.T @ W) + f64(base), 0.0)
    C = mxq(H, 1, "e4m3") @ mxq(f64(recipe), 0, "e4m3")
    y = np.maximum(C + f64(safety), f64(lot)) * f64(share)
    Y = y.T
    words, scales = planes(Y)
    return y, words, scales

@@ -1,0 +1,292 @@
+from contextlib import ExitStack
+
+import concourse.mybir as mybir
+from concourse.masks import make_identity
+
+M, T, F, N = 1024, 1024, 1536, 2048
+FLOPS = 2 * M * T * F + 2 * M * F * N
+
+F32 = mybir.dt.float32
+BF16 = mybir.dt.bfloat16
+I32 = mybir.dt.int32
+U8 = mybir.dt.uint8
+FP8X4 = mybir.dt.float8_e4m3fn_x4
+FP4X4 = mybir.dt.float4_e2m1fn_x4
+ACT = mybir.ActivationFunctionType
+ALU = mybir.AluOpType
+
+P = 128
+PACK = 4
+W512 = 512
+TG = T // W512
+FG = F // W512
+NG = N // W512
+MH = M // W512
+
+
+def tile_forecast_recipe_supplier_orders_h2_kernel(
+    tc, x_words, x_scales, w_words, w_scales, base, recipe, safety, lot, share, out_0, out_1, out_2
+):
+    nc = tc.nc
+    with ExitStack() as ctx:
+        keep = ctx.enter_context(tc.tile_pool(name="keep", bufs=1))
+        work = ctx.enter_context(tc.tile_pool(name="work", bufs=2))
+        psum = ctx.enter_context(tc.psum_pool(name="psum", bufs=4))
+        ctx.enter_context(tc.manual_schedule())
+
+        def kept(name, shape, dtype):
+            return keep.tile(shape, dtype, name=name, align_bytes=64)
+
+        x_code = [kept("x_code%d" % h, [P, TG, W512], I32) for h in range(MH)]
+        x_scale = kept("x_scale", [P, TG, M], U8)
+        w_raw0 = kept("w_raw0", [P, TG, 2 * W512], U8)
+        w_raw1 = kept("w_raw1", [P, TG, 4 * W512], U8)
+        w_raw = [w_raw0[:], w_raw1[:, :, 0 : 2 * W512], w_raw1[:, :, 2 * W512 : 4 * W512]]
+        ws_raw = kept("ws_raw", [P, TG, F], U8)
+        w_code = [kept("w_code%d" % f, [P, TG, 2 * W512], U8) for f in range(FG)]
+        w_scale = [kept("w_scale%d" % f, [P, TG, W512], U8) for f in range(FG)]
+        base_raw = kept("base_raw", [P, FG, 16], BF16)
+        base_col = kept("base_col", [P, FG, PACK], F32)
+        safety_col = kept("safety_col", [P, NG, PACK], BF16)
+        lot_col = kept("lot_col", [P, NG, PACK], BF16)
+        share_col = kept("share_col", [P, NG, PACK], BF16)
+        ident = kept("ident", [P, P], F32)
+        r_first = [kept("r_first%d" % f, [P, PACK, W512], BF16) for f in range(FG)]
+        r_rest = [kept("r_rest%d" % f, [P, PACK, N - W512], BF16) for f in range(FG)]
+        r_code = {}
+        r_scale = {}
+        h_code = {}
+        h_scale = {}
+        for f in range(FG):
+            for g in range(NG):
+                r_code[g, f] = kept("r_code%d_%d" % (g, f), [P, W512], I32)
+                r_scale[g, f] = kept("r_scale%d_%d" % (g, f), [P, W512], U8)
+            for h in range(MH):
+                h_code[h, f] = kept("h_code%d_%d" % (h, f), [P, W512], I32)
+                h_scale[h, f] = kept("h_scale%d_%d" % (h, f), [P, W512], U8)
+        y_scale = kept("y_scale", [P, NG, M], U8)
+
+        def load_x(h):
+            src = x_words.rearrange("g p n t -> p g (n t)")[:, :, 4 * W512 * h : 4 * W512 * (h + 1)]
+            nc.sync.dma_start(out=x_code[h][:], in_=src.bitcast(I32))
+
+        def load_scales(eng, plane, scales):
+            for r in range(4):
+                eng.dma_start(
+                    out=plane[r:P:32, :, :].bitcast(I32),
+                    in_=scales[:, r:16:4, :].rearrange("g q n -> q g n").bitcast(I32),
+                )
+
+        def load_recipe(dst, f, c0, c1):
+            rows = recipe[W512 * f : W512 * (f + 1), c0:c1].rearrange("(q j e) n -> e q j n", j=4, e=4)
+            for e in range(4):
+                nc.sync.dma_start(out=dst[e:P:4, :, :], in_=rows[e])
+
+        nc.vector.memset(ws_raw[:].bitcast(I32), 0)
+        nc.vector.memset(x_scale[:].bitcast(I32), 0)
+        base_rows = base.rearrange("(f q s) -> q f s", f=FG, s=16)
+        load_scales(nc.gpsimd, x_scale, x_scales)
+        make_identity(nc, ident[:])
+        w_rows = w_words.rearrange("g p b -> p g b")
+        load_recipe(r_first[0], 0, 0, W512)
+        load_scales(nc.sync, ws_raw, w_scales)
+        nc.sync.dma_start(out=w_raw0[:].bitcast(I32), in_=w_rows[:, :, 0 : 2 * W512].bitcast(I32))
+        load_x(0)
+        for e in range(4):
+            nc.sync.dma_start(out=base_raw[e:P:4, :, 0:13], in_=base_rows[:, :, e : e + 13])
+        nc.sync.dma_start(out=w_raw1[:].bitcast(I32), in_=w_rows[:, :, 2 * W512 : 6 * W512].bitcast(I32))
+        load_recipe(r_first[1], 1, 0, W512)
+        load_recipe(r_first[2], 2, 0, W512)
+        load_x(1)
+        for col, vec in ((safety_col, safety), (lot_col, lot), (share_col, share)):
+            nc.sync.dma_start(out=col[:], in_=vec.rearrange("(g p t) -> p g t", g=NG, t=PACK))
+        for f in range(FG):
+            load_recipe(r_rest[f], f, W512, N)
+
+        nc.scalar.activation(out=base_col[:], in_=base_raw[:, :, 0:13:4], func=ACT.Identity)
+
+        def permute_w(f):
+            nc.vector.tensor_copy(
+                out=w_code[f][:].bitcast(I32).rearrange("p g (t q w) -> p g t q w", t=4, w=2),
+                in_=w_raw[f].bitcast(I32).rearrange("p g (q t w) -> p g t q w", t=4, w=2),
+            )
+            nc.vector.tensor_copy(
+                out=w_scale[f][:].bitcast(I32).rearrange("p g (t q) -> p g t q", t=4),
+                in_=ws_raw[:, :, W512 * f : W512 * (f + 1)].bitcast(I32).rearrange("p g (q t) -> p g t q", t=4),
+            )
+
+        grouped = {}
+
+        def group_recipe(g, f):
+            raw = r_first[f][:] if g == 0 else r_rest[f][:, :, W512 * (g - 1) : W512 * g]
+            dst = work.tile([P, PACK * W512], BF16, name="grouped", bufs=3, align_bytes=64)
+            nc.vector.tensor_copy(
+                out=dst[:].rearrange("p (t a m j) -> p t a j m", t=4, m=2, j=4),
+                in_=raw.rearrange("p j (a m t) -> p t a j m", m=2, t=4),
+            )
+            grouped["r", g, f] = dst
+
+        def group_rows(key, src):
+            dst = work.tile([P, PACK * W512], BF16, name="grouped", bufs=3, align_bytes=64)
+            nc.vector.tensor_copy(
+                out=dst[:].rearrange("p (c i t) -> p c t i", i=4, t=4),
+                in_=src[:].rearrange("p t (c i) -> p c t i", i=4),
+            )
+            grouped[key] = dst
+
+        def quant(key, codes, scales):
+            nc.vector.quantize_mx(out=codes.bitcast(FP8X4), scales=scales, in_=grouped[key][:])
+
+        def quant_recipe(g, f):
+            quant(("r", g, f), r_code[g, f][:], r_scale[g, f][:])
+
+        h_rows = {}
+
+        def stage1(i):
+            h, f = divmod(i, FG)
+            rows = work.tile([P, PACK, W512], BF16, name="h_rows", bufs=3, align_bytes=64)
+            for t in range(PACK):
+                acc = psum.tile([P, W512], F32, name="acc")
+                for k in range(TG):
+                    nc.tensor.matmul_mx(
+                        out=acc[:],
+                        lhsT=w_code[f][:, k, 2 * P * t : 2 * P * (t + 1)].bitcast(FP4X4),
+                        lhsT_scale=w_scale[f][:, k, P * t : P * (t + 1)],
+                        rhs=x_code[h][:, k, :].bitcast(FP8X4),
+                        rhs_scale=x_scale[:, k, W512 * h : W512 * (h + 1)],
+                        start=(k == 0),
+                        stop=(k == TG - 1),
+                    )
+                nc.scalar.activation(out=rows[:, t, :], in_=acc[:], func=ACT.Relu, bias=base_col[:, f, t : t + 1])
+            h_rows[i] = rows
+
+        def group_h(i):
+            group_rows(("h", i), h_rows[i])
+
+        def quant_h(i):
+            h, f = divmod(i, FG)
+            quant(("h", i), h_code[h, f][:], h_scale[h, f][:])
+
+        y_rows = {}
+
+        def stage2(u, t):
+            g, h = divmod(u, MH)
+            acc = psum.tile([P, W512], F32, name="acc")
+            for f in range(FG):
+                nc.tensor.matmul_mx(
+                    out=acc[:],
+                    lhsT=r_code[g, f][:, P * t : P * (t + 1)].bitcast(FP8X4),
+                    lhsT_scale=r_scale[g, f][:, P * t : P * (t + 1)],
+                    rhs=h_code[h, f][:].bitcast(FP8X4),
+                    rhs_scale=h_scale[h, f][:],
+                    start=(f == 0),
+                    stop=(f == FG - 1),
+                )
+            if t == 0:
+                y_rows[u] = work.tile([P, PACK, W512], F32, name="y_rows", bufs=6, align_bytes=64)
+            nc.scalar.activation(out=y_rows[u][:, t, :], in_=acc[:], func=ACT.Identity, bias=safety_col[:, g, t : t + 1])
+
+        def finish(u, t):
+            g = u // MH
+            nc.vector.tensor_scalar(
+                out=y_rows[u][:, t, :], in0=y_rows[u][:, t, :],
+                scalar1=lot_col[:, g, t : t + 1], scalar2=share_col[:, g, t : t + 1],
+                op0=ALU.max, op1=ALU.mult,
+            )
+
+        turned = {}
+
+        def turn(u):
+            for s in range(4):
+                bank = psum.tile([P, PACK, P], F32, name="turned")
+                for t in range(PACK):
+                    nc.tensor.transpose(bank[:, t, :], y_rows[u][:, t, P * s : P * (s + 1)], ident[:])
+                turned[u, s] = bank
+
+        y_out = {}
+
+        def drain(u, s):
+            g, h = divmod(u, MH)
+            if s % 2 == 0:
+                y_out[u] = work.tile([P, 2, W512], F32, name="y_out", bufs=4, align_bytes=64)
+            nc.scalar.copy(
+                out=y_out[u][:, s % 2, :].rearrange("p (m t) -> p m t", t=4),
+                in_=turned[u, s][:].rearrange("p t m -> p m t"),
+            )
+            dst = out_0[W512 * h : W512 * (h + 1), W512 * g : W512 * (g + 1)].rearrange("(s p) n -> p s n", p=P)
+            if s % 2 == 1:
+                nc.sync.dma_start(out=dst[:, s - 1 : s + 1, :], in_=y_out[u][:])
+
+        def group_y(u):
+            group_rows(("y", u), y_rows[u])
+
+        y_code = {}
+
+        def quant_y(u):
+            g, h = divmod(u, MH)
+            y_code[u] = work.tile([P, W512], I32, name="y_code", bufs=4, align_bytes=64)
+            quant(("y", u), y_code[u][:], y_scale[:, g, W512 * h : W512 * (h + 1)])
+
+        def store_codes(u):
+            g, h = divmod(u, MH)
+            dst = out_1[g].rearrange("p m t -> p (m t)")[:, 4 * W512 * h : 4 * W512 * (h + 1)]
+            nc.sync.dma_start(out=dst.bitcast(I32), in_=y_code[u][:])
+
+        def store_scales(g0, g1):
+            for r in range(4):
+                nc.sync.dma_start(
+                    out=out_2[g0:g1, r:16:4, :].rearrange("g q n -> q g n").bitcast(I32),
+                    in_=y_scale[r:P:32, g0:g1, :].bitcast(I32),
+                )
+
+        units = NG * MH
+        steps = {"pw": permute_w, "gr": group_recipe, "qr": quant_recipe, "gh": group_h, "qh": quant_h,
+                 "fin": finish, "gy": group_y, "qy": quant_y, "s1": stage1, "s2": stage2, "turn": turn,
+                 "drain": drain, "sc": store_codes, "ss": store_scales}
+
+        def fins(u):
+            return [("fin", u, t) for t in range(PACK)]
+
+        vec_order = [("gr", 0, 0), ("pw", 0), ("qr", 0, 0), ("pw", 1), ("pw", 2), ("gr", 0, 1), ("gh", 0), ("qr", 0, 1),
+                     ("gr", 0, 2), ("qh", 0), ("gh", 1), ("qr", 0, 2), ("gh", 2), ("qh", 1), ("gh", 3), ("qh", 2),
+                     ("gh", 4), ("qh", 3), ("gh", 5), ("qh", 4), ("gr", 1, 0), ("qh", 5)]
+        vec_order += fins(0) + [("qr", 1, 0), ("gr", 1, 1), ("gr", 1, 2), ("qr", 1, 1), ("qr", 1, 2)] + fins(1)
+        vec_order += [("gr", 2, 0), ("gr", 2, 1), ("qr", 2, 0)] + fins(2) + [("qr", 2, 1), ("gr", 2, 2), ("gy", 0), ("qr", 2, 2)]
+        vec_order += fins(3) + [("qy", 0), ("gr", 3, 0), ("gr", 3, 1), ("qr", 3, 0)] + fins(4)
+        vec_order += [("qr", 3, 1), ("gr", 3, 2), ("gy", 1), ("qr", 3, 2)] + fins(5) + [("qy", 1), ("gy", 2), ("gy", 3), ("qy", 2)]
+        vec_order += fins(6) + [("qy", 3), ("gy", 4), ("gy", 5), ("qy", 4)] + fins(7)
+        vec_order += [("qy", 5), ("gy", 6), ("gy", 7), ("qy", 6), ("qy", 7)]
+
+        main = [("s1", i) for i in range(MH * FG)]
+        codes_after = {(4, 2): 0, (6, 2): 1, (7, 0): 2, (7, 2): 3}
+        for u in range(units):
+            for t in range(PACK):
+                main.append(("s2", u, t))
+                if t == 0 and u >= 2:
+                    main.append(("drain", u - 2, 3))
+                if t == 1 and u >= 1:
+                    main.append(("turn", u - 1))
+                if t >= 1 and u >= 1:
+                    main.append(("drain", u - 1, t - 1))
+                if (u, t) in codes_after:
+                    main.append(("sc", codes_after[u, t]))
+        main += [("sc", 4), ("drain", units - 2, 3), ("sc", 5), ("turn", units - 1)]
+        main += [("drain", units - 1, s) for s in range(4)]
+        main += [("sc", 6), ("sc", 7), ("ss", 0, 4)]
+
+        def producer(item):
+            if item[0] == "gh":
+                return ("s1", item[1])
+            if item[0] == "fin":
+                return ("s2", item[1], item[2])
+            return None
+
+        done = set()
+        pos = 0
+        for item in main:
+            while pos < len(vec_order) and (producer(vec_order[pos]) is None or producer(vec_order[pos]) in done):
+                steps[vec_order[pos][0]](*vec_order[pos][1:])
+                pos += 1
+            steps[item[0]](*item[1:])
+            done.add(item)
+        assert pos == len(vec_order)

@@ -39,13 +39,11 @@ def tile_forecast_recipe_supplier_orders_h2_kernel(
 
         x_code = [kept("x_code%d" % h, [P, TG, W512], I32) for h in range(MH)]
         x_scale = kept("x_scale", [P, TG, M], U8)
-        w_raw0 = kept("w_raw0", [P, TG, 2 * W512], U8)
-        w_raw1 = kept("w_raw1", [P, TG, 4 * W512], U8)
-        w_raw = [w_raw0[:], w_raw1[:, :, 0 : 2 * W512], w_raw1[:, :, 2 * W512 : 4 * W512]]
+        w_raw = [kept("w_raw%d" % f, [P, TG, 2 * W512], U8) for f in range(FG)]
         ws_raw = kept("ws_raw", [P, TG, F], U8)
         w_code = [kept("w_code%d" % f, [P, TG, 2 * W512], U8) for f in range(FG)]
         w_scale = [kept("w_scale%d" % f, [P, TG, W512], U8) for f in range(FG)]
-        base_raw = kept("base_raw", [P, FG, 16], BF16)
+        base_raw = kept("base_raw", [P, FG, 8], BF16)
         base_col = kept("base_col", [P, FG, PACK], F32)
         safety_col = kept("safety_col", [P, NG, PACK], BF16)
         lot_col = kept("lot_col", [P, NG, PACK], BF16)
@@ -70,6 +68,10 @@ def tile_forecast_recipe_supplier_orders_h2_kernel(
             src = x_words.rearrange("g p n t -> p g (n t)")[:, :, 4 * W512 * h : 4 * W512 * (h + 1)]
             nc.sync.dma_start(out=x_code[h][:], in_=src.bitcast(I32))
 
+        def load_w(f):
+            src = w_words.rearrange("g p b -> p g b")[:, :, 2 * W512 * f : 2 * W512 * (f + 1)]
+            nc.sync.dma_start(out=w_raw[f][:].bitcast(I32), in_=src.bitcast(I32))
+
         def load_scales(eng, plane, scales):
             for r in range(4):
                 eng.dma_start(
@@ -78,24 +80,24 @@ def tile_forecast_recipe_supplier_orders_h2_kernel(
                 )
 
         def load_recipe(dst, f, c0, c1):
-            rows = recipe[W512 * f : W512 * (f + 1), c0:c1].rearrange("(q j e) n -> e q j n", j=4, e=4)
-            for e in range(4):
-                nc.sync.dma_start(out=dst[e:P:4, :, :], in_=rows[e])
+            rows = recipe[W512 * f : W512 * (f + 1), c0:c1].rearrange("(q j e) n -> e q j n", j=4, e=2)
+            for e in range(2):
+                nc.sync.dma_start(out=dst[e:P:2, :, :], in_=rows[e])
 
         nc.vector.memset(ws_raw[:].bitcast(I32), 0)
         nc.vector.memset(x_scale[:].bitcast(I32), 0)
-        base_rows = base.rearrange("(f q s) -> q f s", f=FG, s=16)
-        load_scales(nc.gpsimd, x_scale, x_scales)
         make_identity(nc, ident[:])
-        w_rows = w_words.rearrange("g p b -> p g b")
+        base_rows = base.rearrange("(f q s) -> q f s", f=FG, s=8)
         load_recipe(r_first[0], 0, 0, W512)
         load_scales(nc.sync, ws_raw, w_scales)
-        nc.sync.dma_start(out=w_raw0[:].bitcast(I32), in_=w_rows[:, :, 0 : 2 * W512].bitcast(I32))
+        load_w(0)
         load_x(0)
-        for e in range(4):
-            nc.sync.dma_start(out=base_raw[e:P:4, :, 0:13], in_=base_rows[:, :, e : e + 13])
-        nc.sync.dma_start(out=w_raw1[:].bitcast(I32), in_=w_rows[:, :, 2 * W512 : 6 * W512].bitcast(I32))
+        load_scales(nc.sync, x_scale, x_scales)
+        for e in range(2):
+            nc.sync.dma_start(out=base_raw[e:P:2, :, 0:7], in_=base_rows[:, :, e : e + 7])
+        load_w(1)
         load_recipe(r_first[1], 1, 0, W512)
+        load_w(2)
         load_recipe(r_first[2], 2, 0, W512)
         load_x(1)
         for col, vec in ((safety_col, safety), (lot_col, lot), (share_col, share)):
@@ -103,39 +105,43 @@ def tile_forecast_recipe_supplier_orders_h2_kernel(
         for f in range(FG):
             load_recipe(r_rest[f], f, W512, N)
 
-        nc.scalar.activation(out=base_col[:], in_=base_raw[:, :, 0:13:4], func=ACT.Identity)
+        nc.scalar.activation(out=base_col[:], in_=base_raw[:, :, 0:7:2], func=ACT.Identity)
 
         def permute_w(f):
             nc.vector.tensor_copy(
-                out=w_code[f][:].bitcast(I32).rearrange("p g (t q w) -> p g t q w", t=4, w=2),
-                in_=w_raw[f].bitcast(I32).rearrange("p g (q t w) -> p g t q w", t=4, w=2),
+                out=w_code[f][:].bitcast(I32).rearrange("p g (t q) -> p g q t", t=4),
+                in_=w_raw[f][:].bitcast(I32).rearrange("p g (q t) -> p g q t", t=4),
             )
+
+        def permute_w_scales(f):
             nc.vector.tensor_copy(
-                out=w_scale[f][:].bitcast(I32).rearrange("p g (t q) -> p g t q", t=4),
-                in_=ws_raw[:, :, W512 * f : W512 * (f + 1)].bitcast(I32).rearrange("p g (q t) -> p g t q", t=4),
+                out=w_scale[f][:].rearrange("p g (t q e) -> p g t q e", t=4, e=2),
+                in_=ws_raw[:, :, W512 * f : W512 * (f + 1)].rearrange("p g (q t e) -> p g t q e", t=4, e=2),
             )
 
         grouped = {}
 
-        def group_recipe(g, f):
+        def staging(key):
+            if key not in grouped:
+                grouped[key] = work.tile([P, PACK * W512], BF16, name="grouped", bufs=4, align_bytes=64)
+            return grouped[key]
+
+        def group_recipe(copy, g, f, lo=0, hi=2):
             raw = r_first[f][:] if g == 0 else r_rest[f][:, :, W512 * (g - 1) : W512 * g]
-            dst = work.tile([P, PACK * W512], BF16, name="grouped", bufs=3, align_bytes=64)
-            nc.vector.tensor_copy(
-                out=dst[:].rearrange("p (t a m j) -> p t a j m", t=4, m=2, j=4),
-                in_=raw.rearrange("p j (a m t) -> p t a j m", m=2, t=4),
+            copy(
+                out=staging(("r", g, f))[:].rearrange("p (t a m j) -> p t a j m", t=4, m=2, j=4)[:, 2 * lo : 2 * hi],
+                in_=raw.rearrange("p j (a m t) -> p t a j m", m=2, t=4)[:, 2 * lo : 2 * hi],
             )
-            grouped["r", g, f] = dst
 
-        def group_rows(key, src):
-            dst = work.tile([P, PACK * W512], BF16, name="grouped", bufs=3, align_bytes=64)
-            nc.vector.tensor_copy(
-                out=dst[:].rearrange("p (c i t) -> p c t i", i=4, t=4),
-                in_=src[:].rearrange("p t (c i) -> p c t i", i=4),
+        def group_rows(copy, key, src, width, lo, hi):
+            c0, c1 = width // 8 * lo, width // 8 * hi
+            copy(
+                out=staging(key)[:, 0 : PACK * width].rearrange("p (c i t) -> p c t i", i=4, t=4)[:, c0:c1],
+                in_=src[:].rearrange("p t (c i) -> p c t i", i=4)[:, c0:c1],
             )
-            grouped[key] = dst
 
-        def quant(key, codes, scales):
-            nc.vector.quantize_mx(out=codes.bitcast(FP8X4), scales=scales, in_=grouped[key][:])
+        def quant(key, codes, scales, width=W512):
+            nc.vector.quantize_mx(out=codes.bitcast(FP8X4), scales=scales, in_=grouped[key][:, 0 : PACK * width])
 
         def quant_recipe(g, f):
             quant(("r", g, f), r_code[g, f][:], r_scale[g, f][:])
@@ -160,34 +166,36 @@ def tile_forecast_recipe_supplier_orders_h2_kernel(
                 nc.scalar.activation(out=rows[:, t, :], in_=acc[:], func=ACT.Relu, bias=base_col[:, f, t : t + 1])
             h_rows[i] = rows
 
-        def group_h(i):
-            group_rows(("h", i), h_rows[i])
+        def group_h(copy, i, lo=0, hi=2):
+            group_rows(copy, ("h", i), h_rows[i], W512, lo, hi)
 
         def quant_h(i):
             h, f = divmod(i, FG)
             quant(("h", i), h_code[h, f][:], h_scale[h, f][:])
 
         y_rows = {}
+        units = [(g, W512 * h, W512) for g in range(NG) for h in range(MH)][:-1] + [(3, 512, 256), (3, 768, 256)]
 
         def stage2(u, t):
-            g, h = divmod(u, MH)
-            acc = psum.tile([P, W512], F32, name="acc")
+            g, m0, width = units[u]
+            h, c0 = divmod(m0, W512)
+            acc = psum.tile([P, width], F32, name="acc")
             for f in range(FG):
                 nc.tensor.matmul_mx(
                     out=acc[:],
                     lhsT=r_code[g, f][:, P * t : P * (t + 1)].bitcast(FP8X4),
                     lhsT_scale=r_scale[g, f][:, P * t : P * (t + 1)],
-                    rhs=h_code[h, f][:].bitcast(FP8X4),
-                    rhs_scale=h_scale[h, f][:],
+                    rhs=h_code[h, f][:, c0 : c0 + width].bitcast(FP8X4),
+                    rhs_scale=h_scale[h, f][:, c0 : c0 + width],
                     start=(f == 0),
                     stop=(f == FG - 1),
                 )
-            if t == 0:
-                y_rows[u] = work.tile([P, PACK, W512], F32, name="y_rows", bufs=6, align_bytes=64)
+            if u not in y_rows:
+                y_rows[u] = work.tile([P, PACK, width], F32, name="y_rows", bufs=6, align_bytes=64)
             nc.scalar.activation(out=y_rows[u][:, t, :], in_=acc[:], func=ACT.Identity, bias=safety_col[:, g, t : t + 1])
 
         def finish(u, t):
-            g = u // MH
+            g = units[u][0]
             nc.vector.tensor_scalar(
                 out=y_rows[u][:, t, :], in0=y_rows[u][:, t, :],
                 scalar1=lot_col[:, g, t : t + 1], scalar2=share_col[:, g, t : t + 1],
@@ -197,7 +205,7 @@ def tile_forecast_recipe_supplier_orders_h2_kernel(
         turned = {}
 
         def turn(u):
-            for s in range(4):
+            for s in range(units[u][2] // P):
                 bank = psum.tile([P, PACK, P], F32, name="turned")
                 for t in range(PACK):
                     nc.tensor.transpose(bank[:, t, :], y_rows[u][:, t, P * s : P * (s + 1)], ident[:])
@@ -205,31 +213,32 @@ def tile_forecast_recipe_supplier_orders_h2_kernel(
 
         y_out = {}
 
-        def drain(u, s):
-            g, h = divmod(u, MH)
-            if s % 2 == 0:
-                y_out[u] = work.tile([P, 2, W512], F32, name="y_out", bufs=4, align_bytes=64)
-            nc.scalar.copy(
-                out=y_out[u][:, s % 2, :].rearrange("p (m t) -> p m t", t=4),
+        def drain(copy, u, s):
+            if (u, s // 2) not in y_out:
+                y_out[u, s // 2] = work.tile([P, 2, W512], F32, name="y_out", bufs=4, align_bytes=64)
+            copy(
+                out=y_out[u, s // 2][:, s % 2, :].rearrange("p (m t) -> p m t", t=4),
                 in_=turned[u, s][:].rearrange("p t m -> p m t"),
             )
-            dst = out_0[W512 * h : W512 * (h + 1), W512 * g : W512 * (g + 1)].rearrange("(s p) n -> p s n", p=P)
-            if s % 2 == 1:
-                nc.sync.dma_start(out=dst[:, s - 1 : s + 1, :], in_=y_out[u][:])
 
-        def group_y(u):
-            group_rows(("y", u), y_rows[u])
+        def store_y(u, k):
+            g, m0, width = units[u]
+            dst = out_0[m0 + 2 * P * k : m0 + 2 * P * (k + 1), W512 * g : W512 * (g + 1)].rearrange("(s p) n -> p s n", p=P)
+            nc.sync.dma_start(out=dst, in_=y_out[u, k][:])
+
+        def group_y(copy, u, lo=0, hi=2):
+            group_rows(copy, ("y", u), y_rows[u], units[u][2], lo, hi)
 
         y_code = {}
 
         def quant_y(u):
-            g, h = divmod(u, MH)
-            y_code[u] = work.tile([P, W512], I32, name="y_code", bufs=4, align_bytes=64)
-            quant(("y", u), y_code[u][:], y_scale[:, g, W512 * h : W512 * (h + 1)])
+            g, m0, width = units[u]
+            y_code[u] = work.tile([P, width], I32, name="y_code", bufs=5, align_bytes=64)
+            quant(("y", u), y_code[u][:], y_scale[:, g, m0 : m0 + width], width)
 
         def store_codes(u):
-            g, h = divmod(u, MH)
-            dst = out_1[g].rearrange("p m t -> p (m t)")[:, 4 * W512 * h : 4 * W512 * (h + 1)]
+            g, m0, width = units[u]
+            dst = out_1[g].rearrange("p m t -> p (m t)")[:, 4 * m0 : 4 * (m0 + width)]
             nc.sync.dma_start(out=dst.bitcast(I32), in_=y_code[u][:])
 
         def store_scales(g0, g1):
@@ -239,54 +248,107 @@ def tile_forecast_recipe_supplier_orders_h2_kernel(
                     in_=y_scale[r:P:32, g0:g1, :].bitcast(I32),
                 )
 
-        units = NG * MH
-        steps = {"pw": permute_w, "gr": group_recipe, "qr": quant_recipe, "gh": group_h, "qh": quant_h,
-                 "fin": finish, "gy": group_y, "qy": quant_y, "s1": stage1, "s2": stage2, "turn": turn,
-                 "drain": drain, "sc": store_codes, "ss": store_scales}
+        vector_copy, scalar_copy = nc.vector.tensor_copy, nc.scalar.copy
 
-        def fins(u):
-            return [("fin", u, t) for t in range(PACK)]
+        def finish_all(u, first=0, last=PACK):
+            for t in range(first, last):
+                finish(u, t)
 
-        vec_order = [("gr", 0, 0), ("pw", 0), ("qr", 0, 0), ("pw", 1), ("pw", 2), ("gr", 0, 1), ("gh", 0), ("qr", 0, 1),
-                     ("gr", 0, 2), ("qh", 0), ("gh", 1), ("qr", 0, 2), ("gh", 2), ("qh", 1), ("gh", 3), ("qh", 2),
-                     ("gh", 4), ("qh", 3), ("gh", 5), ("qh", 4), ("gr", 1, 0), ("qh", 5)]
-        vec_order += fins(0) + [("qr", 1, 0), ("gr", 1, 1), ("gr", 1, 2), ("qr", 1, 1), ("qr", 1, 2)] + fins(1)
-        vec_order += [("gr", 2, 0), ("gr", 2, 1), ("qr", 2, 0)] + fins(2) + [("qr", 2, 1), ("gr", 2, 2), ("gy", 0), ("qr", 2, 2)]
-        vec_order += fins(3) + [("qy", 0), ("gr", 3, 0), ("gr", 3, 1), ("qr", 3, 0)] + fins(4)
-        vec_order += [("qr", 3, 1), ("gr", 3, 2), ("gy", 1), ("qr", 3, 2)] + fins(5) + [("qy", 1), ("gy", 2), ("gy", 3), ("qy", 2)]
-        vec_order += fins(6) + [("qy", 3), ("gy", 4), ("gy", 5), ("qy", 4)] + fins(7)
-        vec_order += [("qy", 5), ("gy", 6), ("gy", 7), ("qy", 6), ("qy", 7)]
+        group_recipe(vector_copy, 0, 0)
+        permute_w(0)
+        permute_w_scales(0)
+        quant_recipe(0, 0)
+        permute_w_scales(1)
+        permute_w(1)
+        permute_w_scales(2)
+        group_recipe(vector_copy, 0, 1)
+        permute_w(2)
+        stage1(0)
+        group_h(vector_copy, 0)
+        quant_recipe(0, 1)
+        group_recipe(vector_copy, 0, 2)
+        quant_h(0)
+        stage1(1)
+        group_h(vector_copy, 1)
+        quant_recipe(0, 2)
+        for i in range(2, MH * FG):
+            stage1(i)
+            group_h(vector_copy, i)
+            quant_h(i - 1)
 
-        main = [("s1", i) for i in range(MH * FG)]
-        codes_after = {(4, 2): 0, (6, 2): 1, (7, 0): 2, (7, 2): 3}
-        for u in range(units):
-            for t in range(PACK):
-                main.append(("s2", u, t))
-                if t == 0 and u >= 2:
-                    main.append(("drain", u - 2, 3))
-                if t == 1 and u >= 1:
-                    main.append(("turn", u - 1))
-                if t >= 1 and u >= 1:
-                    main.append(("drain", u - 1, t - 1))
-                if (u, t) in codes_after:
-                    main.append(("sc", codes_after[u, t]))
-        main += [("sc", 4), ("drain", units - 2, 3), ("sc", 5), ("turn", units - 1)]
-        main += [("drain", units - 1, s) for s in range(4)]
-        main += [("sc", 6), ("sc", 7), ("ss", 0, 4)]
+        group_recipe(scalar_copy, 1, 0, 0, 1)
+        stage2(0, 0)
+        finish(0, 0)
+        quant_h(MH * FG - 1)
+        stage2(0, 1)
+        group_recipe(scalar_copy, 1, 0, 1, 2)
+        quant_recipe(1, 0)
+        group_recipe(vector_copy, 1, 2)
+        stage2(0, 2)
+        group_recipe(scalar_copy, 1, 1, 0, 1)
+        stage2(0, 3)
+        finish_all(0, 1)
+        quant_recipe(1, 2)
+        group_recipe(vector_copy, 2, 0)
+        stage2(1, 0)
+        group_recipe(scalar_copy, 1, 1, 1, 2)
+        quant_recipe(1, 1)
 
-        def producer(item):
-            if item[0] == "gh":
-                return ("s1", item[1])
-            if item[0] == "fin":
-                return ("s2", item[1], item[2])
-            return None
+        def vector_work(u):
+            if u == 1:
+                finish_all(1)
+                quant_recipe(2, 0)
+                group_recipe(vector_copy, 2, 1)
+            elif u == 2:
+                finish_all(2, 0, 2)
+                quant_recipe(2, 1)
+                group_recipe(vector_copy, 2, 2)
+                finish_all(2, 2)
+                quant_recipe(2, 2)
+                group_recipe(vector_copy, 3, 0)
+            elif u == 3:
+                finish_all(3, 0, 2)
+                quant_recipe(3, 0)
+                group_recipe(vector_copy, 3, 1)
+                finish_all(3, 2)
+                quant_recipe(3, 1)
+                group_recipe(vector_copy, 3, 2)
+                group_y(vector_copy, 0)
+                quant_recipe(3, 2)
+            elif u in (4, 5):
+                finish_all(u)
+                quant_y(2 * u - 8)
+                group_y(vector_copy, 2 * u - 7)
+                group_y(vector_copy, 2 * u - 6)
+                quant_y(2 * u - 7)
+            else:
+                finish_all(u)
+                quant_y(u - 2)
+                group_y(vector_copy, u - 1)
 
-        done = set()
-        pos = 0
-        for item in main:
-            while pos < len(vec_order) and (producer(vec_order[pos]) is None or producer(vec_order[pos]) in done):
-                steps[vec_order[pos][0]](*vec_order[pos][1:])
-                pos += 1
-            steps[item[0]](*item[1:])
-            done.add(item)
-        assert pos == len(vec_order)
+        codes_ready = {5: [0], 6: [1, 2], 7: [3, 4], 8: [5]}
+        last = len(units) - 1
+        for u in range(1, last + 1):
+            for t in range(1 if u == 1 else 0, PACK):
+                stage2(u, t)
+            for v in codes_ready.get(u, []):
+                store_codes(v)
+            if u == last:
+                store_scales(0, NG - 1)
+            vector_work(u)
+            turn(u - 1)
+            for s in range(units[u - 1][2] // P):
+                drain(scalar_copy, u - 1, s)
+                if s % 2 == 1:
+                    store_y(u - 1, s // 2)
+        store_codes(last - 2)
+        turn(last)
+        drain(scalar_copy, last, 0)
+        drain(scalar_copy, last, 1)
+        group_y(vector_copy, last)
+        quant_y(last - 1)
+        quant_y(last)
+        store_y(last, 0)
+        store_codes(last - 1)
+        store_codes(last)
+        store_scales(NG - 1, NG)

@@ -35,7 +35,7 @@ def tile_forecast_recipe_supplier_orders_h2_kernel(
         ctx.enter_context(tc.manual_schedule())
 
         def kept(name, shape, dtype):
-            return keep.tile(shape, dtype, name=name, align_bytes=64)
+            return keep.tile(shape, dtype, name=name, align_bytes=256)
 
         x_code = [kept("x_code%d" % h, [P, TG, W512], I32) for h in range(MH)]
         x_scale = kept("x_scale", [P, TG, M], U8)
@@ -51,18 +51,12 @@ def tile_forecast_recipe_supplier_orders_h2_kernel(
         ident = kept("ident", [P, P], F32)
         r_first = [kept("r_first%d" % f, [P, PACK, W512], BF16) for f in range(FG)]
         r_rest = [kept("r_rest%d" % f, [P, PACK, N - W512], BF16) for f in range(FG)]
-        r_code = {}
-        r_scale = {}
-        h_code = {}
-        h_scale = {}
-        for f in range(FG):
-            for g in range(NG):
-                r_code[g, f] = kept("r_code%d_%d" % (g, f), [P, W512], I32)
-                r_scale[g, f] = kept("r_scale%d_%d" % (g, f), [P, W512], U8)
-            for h in range(MH):
-                h_code[h, f] = kept("h_code%d_%d" % (h, f), [P, W512], I32)
-                h_scale[h, f] = kept("h_scale%d_%d" % (h, f), [P, W512], U8)
-        y_scale = kept("y_scale", [P, NG, M], U8)
+        r_code = kept("r_code", [P, NG, FG, W512], I32)
+        r_scale = kept("r_scale", [P, NG, FG, W512], U8)
+        h_code = kept("h_code", [P, MH, FG, W512], I32)
+        h_scale = kept("h_scale", [P, MH, FG, W512], U8)
+        y_scale_early = kept("y_scale_early", [P, NG - 1, M], U8)
+        y_scale_last = kept("y_scale_last", [P, 1, M], U8)
 
         def load_x(h):
             src = x_words.rearrange("g p n t -> p g (n t)")[:, :, 4 * W512 * h : 4 * W512 * (h + 1)]
@@ -123,7 +117,7 @@ def tile_forecast_recipe_supplier_orders_h2_kernel(
 
         def staging(key):
             if key not in grouped:
-                grouped[key] = work.tile([P, PACK * W512], BF16, name="grouped", bufs=4, align_bytes=64)
+                grouped[key] = work.tile([P, PACK * W512], BF16, name="grouped", bufs=4, align_bytes=256)
             return grouped[key]
 
         def group_recipe(copy, g, f, lo=0, hi=2):
@@ -144,13 +138,13 @@ def tile_forecast_recipe_supplier_orders_h2_kernel(
             nc.vector.quantize_mx(out=codes.bitcast(FP8X4), scales=scales, in_=grouped[key][:, 0 : PACK * width])
 
         def quant_recipe(g, f):
-            quant(("r", g, f), r_code[g, f][:], r_scale[g, f][:])
+            quant(("r", g, f), r_code[:, g, f, :], r_scale[:, g, f, :])
 
         h_rows = {}
 
         def stage1(i):
             h, f = divmod(i, FG)
-            rows = work.tile([P, PACK, W512], BF16, name="h_rows", bufs=3, align_bytes=64)
+            rows = work.tile([P, PACK, W512], BF16, name="h_rows", bufs=3, align_bytes=256)
             for t in range(PACK):
                 acc = psum.tile([P, W512], F32, name="acc")
                 for k in range(TG):
@@ -171,7 +165,7 @@ def tile_forecast_recipe_supplier_orders_h2_kernel(
 
         def quant_h(i):
             h, f = divmod(i, FG)
-            quant(("h", i), h_code[h, f][:], h_scale[h, f][:])
+            quant(("h", i), h_code[:, h, f, :], h_scale[:, h, f, :])
 
         y_rows = {}
         units = [(g, W512 * h, W512) for g in range(NG) for h in range(MH)][:-1] + [(3, 512, 256), (3, 768, 256)]
@@ -183,15 +177,15 @@ def tile_forecast_recipe_supplier_orders_h2_kernel(
             for f in range(FG):
                 nc.tensor.matmul_mx(
                     out=acc[:],
-                    lhsT=r_code[g, f][:, P * t : P * (t + 1)].bitcast(FP8X4),
-                    lhsT_scale=r_scale[g, f][:, P * t : P * (t + 1)],
-                    rhs=h_code[h, f][:, c0 : c0 + width].bitcast(FP8X4),
-                    rhs_scale=h_scale[h, f][:, c0 : c0 + width],
+                    lhsT=r_code[:, g, f, P * t : P * (t + 1)].bitcast(FP8X4),
+                    lhsT_scale=r_scale[:, g, f, P * t : P * (t + 1)],
+                    rhs=h_code[:, h, f, c0 : c0 + width].bitcast(FP8X4),
+                    rhs_scale=h_scale[:, h, f, c0 : c0 + width],
                     start=(f == 0),
                     stop=(f == FG - 1),
                 )
             if u not in y_rows:
-                y_rows[u] = work.tile([P, PACK, width], F32, name="y_rows", bufs=6, align_bytes=64)
+                y_rows[u] = work.tile([P, PACK, width], F32, name="y_rows", bufs=6, align_bytes=256)
             nc.scalar.activation(out=y_rows[u][:, t, :], in_=acc[:], func=ACT.Identity, bias=safety_col[:, g, t : t + 1])
 
         def finish(u, t):
@@ -215,7 +209,7 @@ def tile_forecast_recipe_supplier_orders_h2_kernel(
 
         def drain(copy, u, s):
             if (u, s // 2) not in y_out:
-                y_out[u, s // 2] = work.tile([P, 2, W512], F32, name="y_out", bufs=4, align_bytes=64)
+                y_out[u, s // 2] = work.tile([P, 2, W512], F32, name="y_out", bufs=4, align_bytes=256)
             copy(
                 out=y_out[u, s // 2][:, s % 2, :].rearrange("p (m t) -> p m t", t=4),
                 in_=turned[u, s][:].rearrange("p t m -> p m t"),
@@ -233,8 +227,9 @@ def tile_forecast_recipe_supplier_orders_h2_kernel(
 
         def quant_y(u):
             g, m0, width = units[u]
-            y_code[u] = work.tile([P, width], I32, name="y_code", bufs=5, align_bytes=64)
-            quant(("y", u), y_code[u][:], y_scale[:, g, m0 : m0 + width], width)
+            y_code[u] = work.tile([P, width], I32, name="y_code", bufs=5, align_bytes=256)
+            plane = y_scale_early[:, g, :] if g < NG - 1 else y_scale_last[:, 0, :]
+            quant(("y", u), y_code[u][:], plane[:, m0 : m0 + width], width)
 
         def store_codes(u):
             g, m0, width = units[u]
@@ -242,10 +237,11 @@ def tile_forecast_recipe_supplier_orders_h2_kernel(
             nc.sync.dma_start(out=dst.bitcast(I32), in_=y_code[u][:])
 
         def store_scales(g0, g1):
+            plane = y_scale_early if g0 == 0 else y_scale_last
             for r in range(4):
                 nc.sync.dma_start(
                     out=out_2[g0:g1, r:16:4, :].rearrange("g q n -> q g n").bitcast(I32),
-                    in_=y_scale[r:P:32, g0:g1, :].bitcast(I32),
+                    in_=plane[r:P:32, :, :].bitcast(I32),
                 )
 
         vector_copy, scalar_copy = nc.vector.tensor_copy, nc.scalar.copy

@@ -16,12 +16,27 @@ ACT = mybir.ActivationFunctionType
 ALU = mybir.AluOpType
 
 P = 128
-PACK = 4
-W512 = 512
-TG = T // W512
-FG = F // W512
-NG = N // W512
-MH = M // W512
+SLOTS = 4
+GROUP = P * SLOTS
+T_PASSES = T // GROUP
+F_PASSES = F // GROUP
+N_GROUPS = N // GROUP
+M_HALVES = M // GROUP
+ALIGN = 256
+
+H_PIECES = M_HALVES * F_PASSES
+UNITS = [(g, GROUP * h, GROUP) for g in range(N_GROUPS) for h in range(M_HALVES)][:-1] + [
+    (N_GROUPS - 1, GROUP, GROUP // 2),
+    (N_GROUPS - 1, GROUP + GROUP // 2, GROUP // 2),
+]
+LAST = len(UNITS) - 1
+
+H_ROWS_BUFS = 3
+GROUPED_BUFS = 4
+Y_ROWS_BUFS = 6
+Y_OUT_BUFS = 4
+Y_CODE_BUFS = 5
+BANKS_PER_ROLE = 4
 
 
 def tile_forecast_recipe_supplier_orders_h2_kernel(
@@ -31,320 +46,309 @@ def tile_forecast_recipe_supplier_orders_h2_kernel(
     with ExitStack() as ctx:
         keep = ctx.enter_context(tc.tile_pool(name="keep", bufs=1))
         work = ctx.enter_context(tc.tile_pool(name="work", bufs=2))
-        psum = ctx.enter_context(tc.psum_pool(name="psum", bufs=4))
+        psum = ctx.enter_context(tc.psum_pool(name="psum", bufs=BANKS_PER_ROLE))
         ctx.enter_context(tc.manual_schedule())
 
         def kept(name, shape, dtype):
-            return keep.tile(shape, dtype, name=name, align_bytes=256)
+            return keep.tile(shape, dtype, name=name, align_bytes=ALIGN)
 
-        x_code = [kept("x_code%d" % h, [P, TG, W512], I32) for h in range(MH)]
-        x_scale = kept("x_scale", [P, TG, M], U8)
-        w_raw = [kept("w_raw%d" % f, [P, TG, 2 * W512], U8) for f in range(FG)]
-        ws_raw = kept("ws_raw", [P, TG, F], U8)
-        w_code = [kept("w_code%d" % f, [P, TG, 2 * W512], U8) for f in range(FG)]
-        w_scale = [kept("w_scale%d" % f, [P, TG, W512], U8) for f in range(FG)]
-        base_raw = kept("base_raw", [P, FG, 8], BF16)
-        base_col = kept("base_col", [P, FG, PACK], F32)
-        safety_col = kept("safety_col", [P, NG, PACK], BF16)
-        lot_col = kept("lot_col", [P, NG, PACK], BF16)
-        share_col = kept("share_col", [P, NG, PACK], BF16)
+        x_code = [kept("x_code%d" % h, [P, T_PASSES, GROUP], I32) for h in range(M_HALVES)]
+        x_scale = kept("x_scale", [P, T_PASSES, M], U8)
+        w_raw = [kept("w_raw%d" % f, [P, T_PASSES, 2 * GROUP], U8) for f in range(F_PASSES)]
+        w_scale_raw = kept("w_scale_raw", [P, T_PASSES, F], U8)
+        w_code = [kept("w_code%d" % f, [P, T_PASSES, 2 * GROUP], U8) for f in range(F_PASSES)]
+        w_scale = [kept("w_scale%d" % f, [P, T_PASSES, GROUP], U8) for f in range(F_PASSES)]
+        base_raw = kept("base_raw", [P, F_PASSES, 8], BF16)
+        base_col = kept("base_col", [P, F_PASSES, SLOTS], F32)
+        safety_col = kept("safety_col", [P, N_GROUPS, SLOTS], BF16)
+        lot_col = kept("lot_col", [P, N_GROUPS, SLOTS], BF16)
+        share_col = kept("share_col", [P, N_GROUPS, SLOTS], BF16)
         ident = kept("ident", [P, P], F32)
-        r_first = [kept("r_first%d" % f, [P, PACK, W512], BF16) for f in range(FG)]
-        r_rest = [kept("r_rest%d" % f, [P, PACK, N - W512], BF16) for f in range(FG)]
-        r_code = kept("r_code", [P, NG, FG, W512], I32)
-        r_scale = kept("r_scale", [P, NG, FG, W512], U8)
-        h_code = kept("h_code", [P, MH, FG, W512], I32)
-        h_scale = kept("h_scale", [P, MH, FG, W512], U8)
-        y_scale_early = kept("y_scale_early", [P, NG - 1, M], U8)
+        r_first = [kept("r_first%d" % f, [P, SLOTS, GROUP], BF16) for f in range(F_PASSES)]
+        r_rest = [kept("r_rest%d" % f, [P, SLOTS, N - GROUP], BF16) for f in range(F_PASSES)]
+        r_code = kept("r_code", [P, N_GROUPS, F_PASSES, GROUP], I32)
+        r_scale = kept("r_scale", [P, N_GROUPS, F_PASSES, GROUP], U8)
+        h_code = kept("h_code", [P, M_HALVES, F_PASSES, GROUP], I32)
+        h_scale = kept("h_scale", [P, M_HALVES, F_PASSES, GROUP], U8)
+        y_scale_early = kept("y_scale_early", [P, N_GROUPS - 1, M], U8)
         y_scale_last = kept("y_scale_last", [P, 1, M], U8)
 
         def load_x(h):
-            src = x_words.rearrange("g p n t -> p g (n t)")[:, :, 4 * W512 * h : 4 * W512 * (h + 1)]
+            src = x_words.rearrange("k p n j -> p k (n j)")[:, :, SLOTS * GROUP * h : SLOTS * GROUP * (h + 1)]
             nc.sync.dma_start(out=x_code[h][:], in_=src.bitcast(I32))
 
         def load_w(f):
-            src = w_words.rearrange("g p b -> p g b")[:, :, 2 * W512 * f : 2 * W512 * (f + 1)]
+            src = w_words.rearrange("k p b -> p k b")[:, :, 2 * GROUP * f : 2 * GROUP * (f + 1)]
             nc.sync.dma_start(out=w_raw[f][:].bitcast(I32), in_=src.bitcast(I32))
 
-        def load_scales(eng, plane, scales):
+        def load_scales(dst, scales):
             for r in range(4):
-                eng.dma_start(
-                    out=plane[r:P:32, :, :].bitcast(I32),
-                    in_=scales[:, r:16:4, :].rearrange("g q n -> q g n").bitcast(I32),
+                nc.sync.dma_start(
+                    out=dst[r:P:32, :, :].bitcast(I32),
+                    in_=scales[:, r:16:4, :].rearrange("k q n -> q k n").bitcast(I32),
                 )
 
-        def load_recipe(dst, f, c0, c1):
-            rows = recipe[W512 * f : W512 * (f + 1), c0:c1].rearrange("(q j e) n -> e q j n", j=4, e=2)
+        def load_recipe(dst, f, col0, col1):
+            rows = recipe[GROUP * f : GROUP * (f + 1), col0:col1].rearrange("(q j e) n -> e q j n", j=SLOTS, e=2)
             for e in range(2):
                 nc.sync.dma_start(out=dst[e:P:2, :, :], in_=rows[e])
 
-        nc.vector.memset(ws_raw[:].bitcast(I32), 0)
+        nc.vector.memset(w_scale_raw[:].bitcast(I32), 0)
         nc.vector.memset(x_scale[:].bitcast(I32), 0)
         make_identity(nc, ident[:])
-        base_rows = base.rearrange("(f q s) -> q f s", f=FG, s=8)
-        load_recipe(r_first[0], 0, 0, W512)
-        load_scales(nc.sync, ws_raw, w_scales)
+
+        load_recipe(r_first[0], 0, 0, GROUP)
+        load_scales(w_scale_raw, w_scales)
         load_w(0)
         load_x(0)
-        load_scales(nc.sync, x_scale, x_scales)
+        load_scales(x_scale, x_scales)
+        base_rows = base.rearrange("(f q s) -> q f s", f=F_PASSES, s=8)
         for e in range(2):
             nc.sync.dma_start(out=base_raw[e:P:2, :, 0:7], in_=base_rows[:, :, e : e + 7])
         load_w(1)
-        load_recipe(r_first[1], 1, 0, W512)
+        load_recipe(r_first[1], 1, 0, GROUP)
         load_w(2)
-        load_recipe(r_first[2], 2, 0, W512)
+        load_recipe(r_first[2], 2, 0, GROUP)
         load_x(1)
         for col, vec in ((safety_col, safety), (lot_col, lot), (share_col, share)):
-            nc.sync.dma_start(out=col[:], in_=vec.rearrange("(g p t) -> p g t", g=NG, t=PACK))
-        for f in range(FG):
-            load_recipe(r_rest[f], f, W512, N)
+            nc.sync.dma_start(out=col[:], in_=vec.rearrange("(g p j) -> p g j", g=N_GROUPS, j=SLOTS))
+        for f in range(F_PASSES):
+            load_recipe(r_rest[f], f, GROUP, N)
 
         nc.scalar.activation(out=base_col[:], in_=base_raw[:, :, 0:7:2], func=ACT.Identity)
 
-        def permute_w(f):
+        def order_w_codes(f):
             nc.vector.tensor_copy(
-                out=w_code[f][:].bitcast(I32).rearrange("p g (t q) -> p g q t", t=4),
-                in_=w_raw[f][:].bitcast(I32).rearrange("p g (q t) -> p g q t", t=4),
+                out=w_code[f][:].bitcast(I32).rearrange("p k (j q) -> p k q j", j=SLOTS),
+                in_=w_raw[f][:].bitcast(I32).rearrange("p k (q j) -> p k q j", j=SLOTS),
             )
 
-        def permute_w_scales(f):
+        def order_w_scales(f):
+            cols = w_scale_raw[:, :, GROUP * f : GROUP * (f + 1)]
             nc.vector.tensor_copy(
-                out=w_scale[f][:].rearrange("p g (t q e) -> p g t q e", t=4, e=2),
-                in_=ws_raw[:, :, W512 * f : W512 * (f + 1)].rearrange("p g (q t e) -> p g t q e", t=4, e=2),
+                out=w_scale[f][:].rearrange("p k (j q e) -> p k j q e", j=SLOTS, e=2),
+                in_=cols.rearrange("p k (q j e) -> p k j q e", j=SLOTS, e=2),
             )
 
         grouped = {}
 
-        def staging(key):
+        def grouped_tile(key):
             if key not in grouped:
-                grouped[key] = work.tile([P, PACK * W512], BF16, name="grouped", bufs=4, align_bytes=256)
+                grouped[key] = work.tile(
+                    [P, SLOTS * GROUP], BF16, name="grouped", bufs=GROUPED_BUFS, align_bytes=ALIGN
+                )
             return grouped[key]
 
-        def group_recipe(copy, g, f, lo=0, hi=2):
-            raw = r_first[f][:] if g == 0 else r_rest[f][:, :, W512 * (g - 1) : W512 * g]
+        def group_recipe(g, f, copy=nc.vector.tensor_copy, c0=0, c1=SLOTS):
+            raw = r_first[f][:] if g == 0 else r_rest[f][:, :, GROUP * (g - 1) : GROUP * g]
+            dst = grouped_tile(("recipe", g, f))
             copy(
-                out=staging(("r", g, f))[:].rearrange("p (t a m j) -> p t a j m", t=4, m=2, j=4)[:, 2 * lo : 2 * hi],
-                in_=raw.rearrange("p j (a m t) -> p t a j m", m=2, t=4)[:, 2 * lo : 2 * hi],
+                out=dst[:].rearrange("p (c a b j) -> p c a j b", c=SLOTS, b=2, j=SLOTS)[:, c0:c1],
+                in_=raw.rearrange("p j (a b c) -> p c a j b", b=2, c=SLOTS)[:, c0:c1],
             )
 
-        def group_rows(copy, key, src, width, lo, hi):
-            c0, c1 = width // 8 * lo, width // 8 * hi
-            copy(
-                out=staging(key)[:, 0 : PACK * width].rearrange("p (c i t) -> p c t i", i=4, t=4)[:, c0:c1],
-                in_=src[:].rearrange("p t (c i) -> p c t i", i=4)[:, c0:c1],
+        def group_rows(key, rows, sites):
+            nc.vector.tensor_copy(
+                out=grouped_tile(key)[:, 0 : SLOTS * sites].rearrange("p (a i j) -> p a j i", i=4, j=SLOTS),
+                in_=rows[:].rearrange("p j (a i) -> p a j i", i=4),
             )
 
-        def quant(key, codes, scales, width=W512):
-            nc.vector.quantize_mx(out=codes.bitcast(FP8X4), scales=scales, in_=grouped[key][:, 0 : PACK * width])
+        def quantise(key, codes, scales, columns):
+            nc.vector.quantize_mx(out=codes.bitcast(FP8X4), scales=scales, in_=grouped[key][:, 0 : SLOTS * columns])
 
-        def quant_recipe(g, f):
-            quant(("r", g, f), r_code[:, g, f, :], r_scale[:, g, f, :])
+        def quantise_recipe(g, f):
+            quantise(("recipe", g, f), r_code[:, g, f, :], r_scale[:, g, f, :], GROUP)
 
         h_rows = {}
 
         def stage1(i):
-            h, f = divmod(i, FG)
-            rows = work.tile([P, PACK, W512], BF16, name="h_rows", bufs=3, align_bytes=256)
-            for t in range(PACK):
-                acc = psum.tile([P, W512], F32, name="acc")
-                for k in range(TG):
+            h, f = divmod(i, F_PASSES)
+            h_rows[i] = work.tile([P, SLOTS, GROUP], BF16, name="h_rows", bufs=H_ROWS_BUFS, align_bytes=ALIGN)
+            for j in range(SLOTS):
+                acc = psum.tile([P, GROUP], F32, name="acc")
+                for k in range(T_PASSES):
                     nc.tensor.matmul_mx(
                         out=acc[:],
-                        lhsT=w_code[f][:, k, 2 * P * t : 2 * P * (t + 1)].bitcast(FP4X4),
-                        lhsT_scale=w_scale[f][:, k, P * t : P * (t + 1)],
+                        lhsT=w_code[f][:, k, 2 * P * j : 2 * P * (j + 1)].bitcast(FP4X4),
+                        lhsT_scale=w_scale[f][:, k, P * j : P * (j + 1)],
                         rhs=x_code[h][:, k, :].bitcast(FP8X4),
-                        rhs_scale=x_scale[:, k, W512 * h : W512 * (h + 1)],
+                        rhs_scale=x_scale[:, k, GROUP * h : GROUP * (h + 1)],
                         start=(k == 0),
-                        stop=(k == TG - 1),
+                        stop=(k == T_PASSES - 1),
                     )
-                nc.scalar.activation(out=rows[:, t, :], in_=acc[:], func=ACT.Relu, bias=base_col[:, f, t : t + 1])
-            h_rows[i] = rows
+                nc.scalar.activation(
+                    out=h_rows[i][:, j, :], in_=acc[:], func=ACT.Relu, bias=base_col[:, f, j : j + 1]
+                )
 
-        def group_h(copy, i, lo=0, hi=2):
-            group_rows(copy, ("h", i), h_rows[i], W512, lo, hi)
+        def group_h(i):
+            group_rows(("h", i), h_rows[i], GROUP)
 
-        def quant_h(i):
-            h, f = divmod(i, FG)
-            quant(("h", i), h_code[:, h, f, :], h_scale[:, h, f, :])
+        def quantise_h(i):
+            h, f = divmod(i, F_PASSES)
+            quantise(("h", i), h_code[:, h, f, :], h_scale[:, h, f, :], GROUP)
 
         y_rows = {}
-        units = [(g, W512 * h, W512) for g in range(NG) for h in range(MH)][:-1] + [(3, 512, 256), (3, 768, 256)]
 
-        def stage2(u, t):
-            g, m0, width = units[u]
-            h, c0 = divmod(m0, W512)
-            acc = psum.tile([P, width], F32, name="acc")
-            for f in range(FG):
+        def stage2(u, j):
+            g, site0, sites = UNITS[u]
+            h, first = divmod(site0, GROUP)
+            acc = psum.tile([P, sites], F32, name="acc")
+            for f in range(F_PASSES):
                 nc.tensor.matmul_mx(
                     out=acc[:],
-                    lhsT=r_code[:, g, f, P * t : P * (t + 1)].bitcast(FP8X4),
-                    lhsT_scale=r_scale[:, g, f, P * t : P * (t + 1)],
-                    rhs=h_code[:, h, f, c0 : c0 + width].bitcast(FP8X4),
-                    rhs_scale=h_scale[:, h, f, c0 : c0 + width],
+                    lhsT=r_code[:, g, f, P * j : P * (j + 1)].bitcast(FP8X4),
+                    lhsT_scale=r_scale[:, g, f, P * j : P * (j + 1)],
+                    rhs=h_code[:, h, f, first : first + sites].bitcast(FP8X4),
+                    rhs_scale=h_scale[:, h, f, first : first + sites],
                     start=(f == 0),
-                    stop=(f == FG - 1),
+                    stop=(f == F_PASSES - 1),
                 )
             if u not in y_rows:
-                y_rows[u] = work.tile([P, PACK, width], F32, name="y_rows", bufs=6, align_bytes=256)
-            nc.scalar.activation(out=y_rows[u][:, t, :], in_=acc[:], func=ACT.Identity, bias=safety_col[:, g, t : t + 1])
-
-        def finish(u, t):
-            g = units[u][0]
-            nc.vector.tensor_scalar(
-                out=y_rows[u][:, t, :], in0=y_rows[u][:, t, :],
-                scalar1=lot_col[:, g, t : t + 1], scalar2=share_col[:, g, t : t + 1],
-                op0=ALU.max, op1=ALU.mult,
+                y_rows[u] = work.tile([P, SLOTS, sites], F32, name="y_rows", bufs=Y_ROWS_BUFS, align_bytes=ALIGN)
+            nc.scalar.activation(
+                out=y_rows[u][:, j, :], in_=acc[:], func=ACT.Identity, bias=safety_col[:, g, j : j + 1]
             )
 
-        turned = {}
+        def finish(u, j0=0, j1=SLOTS):
+            g = UNITS[u][0]
+            for j in range(j0, j1):
+                nc.vector.tensor_scalar(
+                    out=y_rows[u][:, j, :],
+                    in0=y_rows[u][:, j, :],
+                    scalar1=lot_col[:, g, j : j + 1],
+                    scalar2=share_col[:, g, j : j + 1],
+                    op0=ALU.max,
+                    op1=ALU.mult,
+                )
 
-        def turn(u):
-            for s in range(units[u][2] // P):
-                bank = psum.tile([P, PACK, P], F32, name="turned")
-                for t in range(PACK):
-                    nc.tensor.transpose(bank[:, t, :], y_rows[u][:, t, P * s : P * (s + 1)], ident[:])
-                turned[u, s] = bank
+        def turn_and_store(u):
+            g, site0, sites = UNITS[u]
+            banks = []
+            for s in range(sites // P):
+                bank = psum.tile([P, SLOTS, P], F32, name="turned")
+                for j in range(SLOTS):
+                    nc.tensor.transpose(bank[:, j, :], y_rows[u][:, j, P * s : P * (s + 1)], ident[:])
+                banks.append(bank)
+            for pair in range(sites // (2 * P)):
+                y_out = work.tile([P, 2, GROUP], F32, name="y_out", bufs=Y_OUT_BUFS, align_bytes=ALIGN)
+                for s in range(2):
+                    nc.scalar.copy(
+                        out=y_out[:, s, :].rearrange("p (m j) -> p m j", j=SLOTS),
+                        in_=banks[2 * pair + s][:].rearrange("p j m -> p m j"),
+                    )
+                rows = out_0[site0 + 2 * P * pair : site0 + 2 * P * (pair + 1), GROUP * g : GROUP * (g + 1)]
+                nc.sync.dma_start(out=rows.rearrange("(s p) n -> p s n", p=P), in_=y_out[:])
 
-        y_out = {}
-
-        def drain(copy, u, s):
-            if (u, s // 2) not in y_out:
-                y_out[u, s // 2] = work.tile([P, 2, W512], F32, name="y_out", bufs=4, align_bytes=256)
-            copy(
-                out=y_out[u, s // 2][:, s % 2, :].rearrange("p (m t) -> p m t", t=4),
-                in_=turned[u, s][:].rearrange("p t m -> p m t"),
-            )
-
-        def store_y(u, k):
-            g, m0, width = units[u]
-            dst = out_0[m0 + 2 * P * k : m0 + 2 * P * (k + 1), W512 * g : W512 * (g + 1)].rearrange("(s p) n -> p s n", p=P)
-            nc.sync.dma_start(out=dst, in_=y_out[u, k][:])
-
-        def group_y(copy, u, lo=0, hi=2):
-            group_rows(copy, ("y", u), y_rows[u], units[u][2], lo, hi)
+        def group_y(u):
+            group_rows(("y", u), y_rows[u], UNITS[u][2])
 
         y_code = {}
 
-        def quant_y(u):
-            g, m0, width = units[u]
-            y_code[u] = work.tile([P, width], I32, name="y_code", bufs=5, align_bytes=256)
-            plane = y_scale_early[:, g, :] if g < NG - 1 else y_scale_last[:, 0, :]
-            quant(("y", u), y_code[u][:], plane[:, m0 : m0 + width], width)
+        def quantise_y(u):
+            g, site0, sites = UNITS[u]
+            y_code[u] = work.tile([P, sites], I32, name="y_code", bufs=Y_CODE_BUFS, align_bytes=ALIGN)
+            scales = y_scale_early[:, g, :] if g < N_GROUPS - 1 else y_scale_last[:, 0, :]
+            quantise(("y", u), y_code[u][:], scales[:, site0 : site0 + sites], sites)
 
         def store_codes(u):
-            g, m0, width = units[u]
-            dst = out_1[g].rearrange("p m t -> p (m t)")[:, 4 * m0 : 4 * (m0 + width)]
+            g, site0, sites = UNITS[u]
+            dst = out_1[g].rearrange("p m j -> p (m j)")[:, SLOTS * site0 : SLOTS * (site0 + sites)]
             nc.sync.dma_start(out=dst.bitcast(I32), in_=y_code[u][:])
 
-        def store_scales(g0, g1):
-            plane = y_scale_early if g0 == 0 else y_scale_last
+        def store_scales(src, g0, g1):
             for r in range(4):
                 nc.sync.dma_start(
                     out=out_2[g0:g1, r:16:4, :].rearrange("g q n -> q g n").bitcast(I32),
-                    in_=plane[r:P:32, :, :].bitcast(I32),
+                    in_=src[r:P:32, :, :].bitcast(I32),
                 )
 
-        vector_copy, scalar_copy = nc.vector.tensor_copy, nc.scalar.copy
 
-        def finish_all(u, first=0, last=PACK):
-            for t in range(first, last):
-                finish(u, t)
-
-        group_recipe(vector_copy, 0, 0)
-        permute_w(0)
-        permute_w_scales(0)
-        quant_recipe(0, 0)
-        permute_w_scales(1)
-        permute_w(1)
-        permute_w_scales(2)
-        group_recipe(vector_copy, 0, 1)
-        permute_w(2)
+        group_recipe(0, 0)
+        order_w_codes(0)
+        order_w_scales(0)
+        quantise_recipe(0, 0)
+        order_w_scales(1)
+        order_w_codes(1)
+        order_w_scales(2)
+        group_recipe(0, 1)
+        order_w_codes(2)
         stage1(0)
-        group_h(vector_copy, 0)
-        quant_recipe(0, 1)
-        group_recipe(vector_copy, 0, 2)
-        quant_h(0)
+        group_h(0)
+        quantise_recipe(0, 1)
+        group_recipe(0, 2)
+        quantise_h(0)
         stage1(1)
-        group_h(vector_copy, 1)
-        quant_recipe(0, 2)
-        for i in range(2, MH * FG):
+        group_h(1)
+        quantise_recipe(0, 2)
+        for i in range(2, H_PIECES):
             stage1(i)
-            group_h(vector_copy, i)
-            quant_h(i - 1)
+            group_h(i)
+            quantise_h(i - 1)
 
-        group_recipe(scalar_copy, 1, 0, 0, 1)
+        group_recipe(1, 0, nc.scalar.copy, 0, SLOTS // 2)
         stage2(0, 0)
-        finish(0, 0)
-        quant_h(MH * FG - 1)
+        finish(0, 0, 1)
+        quantise_h(H_PIECES - 1)
+        group_recipe(1, 1)
         stage2(0, 1)
-        group_recipe(scalar_copy, 1, 0, 1, 2)
-        quant_recipe(1, 0)
-        group_recipe(vector_copy, 1, 2)
+        group_recipe(1, 0, nc.scalar.copy, SLOTS // 2, SLOTS)
+        quantise_recipe(1, 0)
+        group_recipe(1, 2)
+        quantise_recipe(1, 1)
         stage2(0, 2)
-        group_recipe(scalar_copy, 1, 1, 0, 1)
         stage2(0, 3)
-        finish_all(0, 1)
-        quant_recipe(1, 2)
-        group_recipe(vector_copy, 2, 0)
-        stage2(1, 0)
-        group_recipe(scalar_copy, 1, 1, 1, 2)
-        quant_recipe(1, 1)
+        finish(0, 1, SLOTS)
+        quantise_recipe(1, 2)
+        group_recipe(2, 0)
 
         def vector_work(u):
             if u == 1:
-                finish_all(1)
-                quant_recipe(2, 0)
-                group_recipe(vector_copy, 2, 1)
+                finish(1)
+                quantise_recipe(2, 0)
+                group_recipe(2, 1)
             elif u == 2:
-                finish_all(2, 0, 2)
-                quant_recipe(2, 1)
-                group_recipe(vector_copy, 2, 2)
-                finish_all(2, 2)
-                quant_recipe(2, 2)
-                group_recipe(vector_copy, 3, 0)
+                finish(2, 0, 2)
+                quantise_recipe(2, 1)
+                group_recipe(2, 2)
+                finish(2, 2, SLOTS)
+                quantise_recipe(2, 2)
+                group_recipe(3, 0)
             elif u == 3:
-                finish_all(3, 0, 2)
-                quant_recipe(3, 0)
-                group_recipe(vector_copy, 3, 1)
-                finish_all(3, 2)
-                quant_recipe(3, 1)
-                group_recipe(vector_copy, 3, 2)
-                group_y(vector_copy, 0)
-                quant_recipe(3, 2)
+                finish(3, 0, 2)
+                quantise_recipe(3, 0)
+                group_recipe(3, 1)
+                finish(3, 2, SLOTS)
+                quantise_recipe(3, 1)
+                group_recipe(3, 2)
+                group_y(0)
+                quantise_recipe(3, 2)
             elif u in (4, 5):
-                finish_all(u)
-                quant_y(2 * u - 8)
-                group_y(vector_copy, 2 * u - 7)
-                group_y(vector_copy, 2 * u - 6)
-                quant_y(2 * u - 7)
+                behind = 2 * (u - 4)
+                finish(u)
+                quantise_y(behind)
+                group_y(behind + 1)
+                group_y(behind + 2)
+                quantise_y(behind + 1)
             else:
-                finish_all(u)
-                quant_y(u - 2)
-                group_y(vector_copy, u - 1)
+                finish(u)
+                quantise_y(u - 2)
+                group_y(u - 1)
 
-        codes_ready = {5: [0], 6: [1, 2], 7: [3, 4], 8: [5]}
-        last = len(units) - 1
-        for u in range(1, last + 1):
-            for t in range(1 if u == 1 else 0, PACK):
-                stage2(u, t)
-            for v in codes_ready.get(u, []):
+        codes_to_store = {5: [0], 6: [1, 2], 7: [3, 4], 8: [5]}
+        for u in range(1, LAST + 1):
+            for j in range(SLOTS):
+                stage2(u, j)
+            for v in codes_to_store.get(u, []):
                 store_codes(v)
-            if u == last:
-                store_scales(0, NG - 1)
+            if u == LAST:
+                store_scales(y_scale_early, 0, N_GROUPS - 1)
             vector_work(u)
-            turn(u - 1)
-            for s in range(units[u - 1][2] // P):
-                drain(scalar_copy, u - 1, s)
-                if s % 2 == 1:
-                    store_y(u - 1, s // 2)
-        store_codes(last - 2)
-        turn(last)
-        drain(scalar_copy, last, 0)
-        drain(scalar_copy, last, 1)
-        group_y(vector_copy, last)
-        quant_y(last - 1)
-        quant_y(last)
-        store_y(last, 0)
-        store_codes(last - 1)
-        store_codes(last)
-        store_scales(NG - 1, NG)
+            turn_and_store(u - 1)
+        store_codes(LAST - 2)
+        turn_and_store(LAST)
+        group_y(LAST)
+        quantise_y(LAST - 1)
+        quantise_y(LAST)
+        store_codes(LAST - 1)
+        store_codes(LAST)
+        store_scales(y_scale_last, N_GROUPS - 1, N_GROUPS)

from contextlib import ExitStack

import concourse.mybir as mybir
from concourse.masks import make_identity

M, T, F, N = 1024, 1024, 1536, 2048
FLOPS = 2 * M * T * F + 2 * M * F * N

F32 = mybir.dt.float32
BF16 = mybir.dt.bfloat16
I32 = mybir.dt.int32
U8 = mybir.dt.uint8
FP8X4 = mybir.dt.float8_e4m3fn_x4
FP4X4 = mybir.dt.float4_e2m1fn_x4
ACT = mybir.ActivationFunctionType
ALU = mybir.AluOpType

P = 128
SLOTS = 4
GROUP = P * SLOTS
T_PASSES = T // GROUP
F_PASSES = F // GROUP
N_GROUPS = N // GROUP
M_HALVES = M // GROUP
ALIGN = 256

H_PIECES = M_HALVES * F_PASSES
UNITS = [(g, GROUP * h, GROUP) for g in range(N_GROUPS) for h in range(M_HALVES)][:-1] + [
    (N_GROUPS - 1, GROUP, GROUP // 2),
    (N_GROUPS - 1, GROUP + GROUP // 2, GROUP // 2),
]
LAST = len(UNITS) - 1

H_ROWS_BUFS = 3
GROUPED_BUFS = 4
Y_ROWS_BUFS = 6
Y_OUT_BUFS = 4
Y_CODE_BUFS = 5
BANKS_PER_ROLE = 4


def tile_forecast_recipe_supplier_orders_h2_kernel(
    tc, x_words, x_scales, w_words, w_scales, base, recipe, safety, lot, share, out_0, out_1, out_2
):
    nc = tc.nc
    with ExitStack() as ctx:
        keep = ctx.enter_context(tc.tile_pool(name="keep", bufs=1))
        work = ctx.enter_context(tc.tile_pool(name="work", bufs=2))
        psum = ctx.enter_context(tc.psum_pool(name="psum", bufs=BANKS_PER_ROLE))
        ctx.enter_context(tc.manual_schedule())

        def kept(name, shape, dtype):
            return keep.tile(shape, dtype, name=name, align_bytes=ALIGN)

        x_code = [kept("x_code%d" % h, [P, T_PASSES, GROUP], I32) for h in range(M_HALVES)]
        x_scale = kept("x_scale", [P, T_PASSES, M], U8)
        w_raw = [kept("w_raw%d" % f, [P, T_PASSES, 2 * GROUP], U8) for f in range(F_PASSES)]
        w_scale_raw = kept("w_scale_raw", [P, T_PASSES, F], U8)
        w_code = [kept("w_code%d" % f, [P, T_PASSES, 2 * GROUP], U8) for f in range(F_PASSES)]
        w_scale = [kept("w_scale%d" % f, [P, T_PASSES, GROUP], U8) for f in range(F_PASSES)]
        base_raw = kept("base_raw", [P, F_PASSES, 8], BF16)
        base_col = kept("base_col", [P, F_PASSES, SLOTS], F32)
        safety_col = kept("safety_col", [P, N_GROUPS, SLOTS], BF16)
        lot_col = kept("lot_col", [P, N_GROUPS, SLOTS], BF16)
        share_col = kept("share_col", [P, N_GROUPS, SLOTS], BF16)
        ident = kept("ident", [P, P], F32)
        r_first = [kept("r_first%d" % f, [P, SLOTS, GROUP], BF16) for f in range(F_PASSES)]
        r_rest = [kept("r_rest%d" % f, [P, SLOTS, N - GROUP], BF16) for f in range(F_PASSES)]
        r_code = kept("r_code", [P, N_GROUPS, F_PASSES, GROUP], I32)
        r_scale = kept("r_scale", [P, N_GROUPS, F_PASSES, GROUP], U8)
        h_code = kept("h_code", [P, M_HALVES, F_PASSES, GROUP], I32)
        h_scale = kept("h_scale", [P, M_HALVES, F_PASSES, GROUP], U8)
        y_scale_early = kept("y_scale_early", [P, N_GROUPS - 1, M], U8)
        y_scale_last = kept("y_scale_last", [P, 1, M], U8)

        def load_x(h):
            src = x_words.rearrange("k p n j -> p k (n j)")[:, :, SLOTS * GROUP * h : SLOTS * GROUP * (h + 1)]
            nc.sync.dma_start(out=x_code[h][:], in_=src.bitcast(I32))

        def load_w(f):
            src = w_words.rearrange("k p b -> p k b")[:, :, 2 * GROUP * f : 2 * GROUP * (f + 1)]
            nc.sync.dma_start(out=w_raw[f][:].bitcast(I32), in_=src.bitcast(I32))

        def load_scales(dst, scales):
            for r in range(4):
                nc.sync.dma_start(
                    out=dst[r:P:32, :, :].bitcast(I32),
                    in_=scales[:, r:16:4, :].rearrange("k q n -> q k n").bitcast(I32),
                )

        def load_recipe(dst, f, col0, col1):
            rows = recipe[GROUP * f : GROUP * (f + 1), col0:col1].rearrange("(q j e) n -> e q j n", j=SLOTS, e=2)
            for e in range(2):
                nc.sync.dma_start(out=dst[e:P:2, :, :], in_=rows[e])

        nc.vector.memset(w_scale_raw[:].bitcast(I32), 0)
        nc.vector.memset(x_scale[:].bitcast(I32), 0)
        make_identity(nc, ident[:])

        load_recipe(r_first[0], 0, 0, GROUP)
        load_scales(w_scale_raw, w_scales)
        load_w(0)
        load_x(0)
        load_scales(x_scale, x_scales)
        base_rows = base.rearrange("(f q s) -> q f s", f=F_PASSES, s=8)
        for e in range(2):
            nc.sync.dma_start(out=base_raw[e:P:2, :, 0:7], in_=base_rows[:, :, e : e + 7])
        load_w(1)
        load_recipe(r_first[1], 1, 0, GROUP)
        load_w(2)
        load_recipe(r_first[2], 2, 0, GROUP)
        load_x(1)
        for col, vec in ((safety_col, safety), (lot_col, lot), (share_col, share)):
            nc.sync.dma_start(out=col[:], in_=vec.rearrange("(g p j) -> p g j", g=N_GROUPS, j=SLOTS))
        for f in range(F_PASSES):
            load_recipe(r_rest[f], f, GROUP, N)

        nc.scalar.activation(out=base_col[:], in_=base_raw[:, :, 0:7:2], func=ACT.Identity)

        def order_w_codes(f):
            nc.vector.tensor_copy(
                out=w_code[f][:].bitcast(I32).rearrange("p k (j q) -> p k q j", j=SLOTS),
                in_=w_raw[f][:].bitcast(I32).rearrange("p k (q j) -> p k q j", j=SLOTS),
            )

        def order_w_scales(f):
            cols = w_scale_raw[:, :, GROUP * f : GROUP * (f + 1)]
            nc.vector.tensor_copy(
                out=w_scale[f][:].rearrange("p k (j q e) -> p k j q e", j=SLOTS, e=2),
                in_=cols.rearrange("p k (q j e) -> p k j q e", j=SLOTS, e=2),
            )

        grouped = {}

        def grouped_tile(key):
            if key not in grouped:
                grouped[key] = work.tile(
                    [P, SLOTS * GROUP], BF16, name="grouped", bufs=GROUPED_BUFS, align_bytes=ALIGN
                )
            return grouped[key]

        def group_recipe(g, f, copy=nc.vector.tensor_copy, c0=0, c1=SLOTS):
            raw = r_first[f][:] if g == 0 else r_rest[f][:, :, GROUP * (g - 1) : GROUP * g]
            dst = grouped_tile(("recipe", g, f))
            copy(
                out=dst[:].rearrange("p (c a b j) -> p c a j b", c=SLOTS, b=2, j=SLOTS)[:, c0:c1],
                in_=raw.rearrange("p j (a b c) -> p c a j b", b=2, c=SLOTS)[:, c0:c1],
            )

        def group_rows(key, rows, sites):
            nc.vector.tensor_copy(
                out=grouped_tile(key)[:, 0 : SLOTS * sites].rearrange("p (a i j) -> p a j i", i=4, j=SLOTS),
                in_=rows[:].rearrange("p j (a i) -> p a j i", i=4),
            )

        def quantise(key, codes, scales, columns):
            nc.vector.quantize_mx(out=codes.bitcast(FP8X4), scales=scales, in_=grouped[key][:, 0 : SLOTS * columns])

        def quantise_recipe(g, f):
            quantise(("recipe", g, f), r_code[:, g, f, :], r_scale[:, g, f, :], GROUP)

        h_rows = {}

        def stage1(i):
            h, f = divmod(i, F_PASSES)
            h_rows[i] = work.tile([P, SLOTS, GROUP], BF16, name="h_rows", bufs=H_ROWS_BUFS, align_bytes=ALIGN)
            for j in range(SLOTS):
                acc = psum.tile([P, GROUP], F32, name="acc")
                for k in range(T_PASSES):
                    nc.tensor.matmul_mx(
                        out=acc[:],
                        lhsT=w_code[f][:, k, 2 * P * j : 2 * P * (j + 1)].bitcast(FP4X4),
                        lhsT_scale=w_scale[f][:, k, P * j : P * (j + 1)],
                        rhs=x_code[h][:, k, :].bitcast(FP8X4),
                        rhs_scale=x_scale[:, k, GROUP * h : GROUP * (h + 1)],
                        start=(k == 0),
                        stop=(k == T_PASSES - 1),
                    )
                nc.scalar.activation(
                    out=h_rows[i][:, j, :], in_=acc[:], func=ACT.Relu, bias=base_col[:, f, j : j + 1]
                )

        def group_h(i):
            group_rows(("h", i), h_rows[i], GROUP)

        def quantise_h(i):
            h, f = divmod(i, F_PASSES)
            quantise(("h", i), h_code[:, h, f, :], h_scale[:, h, f, :], GROUP)

        y_rows = {}

        def stage2(u, j):
            g, site0, sites = UNITS[u]
            h, first = divmod(site0, GROUP)
            acc = psum.tile([P, sites], F32, name="acc")
            for f in range(F_PASSES):
                nc.tensor.matmul_mx(
                    out=acc[:],
                    lhsT=r_code[:, g, f, P * j : P * (j + 1)].bitcast(FP8X4),
                    lhsT_scale=r_scale[:, g, f, P * j : P * (j + 1)],
                    rhs=h_code[:, h, f, first : first + sites].bitcast(FP8X4),
                    rhs_scale=h_scale[:, h, f, first : first + sites],
                    start=(f == 0),
                    stop=(f == F_PASSES - 1),
                )
            if u not in y_rows:
                y_rows[u] = work.tile([P, SLOTS, sites], F32, name="y_rows", bufs=Y_ROWS_BUFS, align_bytes=ALIGN)
            nc.scalar.activation(
                out=y_rows[u][:, j, :], in_=acc[:], func=ACT.Identity, bias=safety_col[:, g, j : j + 1]
            )

        def finish(u, j0=0, j1=SLOTS):
            g = UNITS[u][0]
            for j in range(j0, j1):
                nc.vector.tensor_scalar(
                    out=y_rows[u][:, j, :],
                    in0=y_rows[u][:, j, :],
                    scalar1=lot_col[:, g, j : j + 1],
                    scalar2=share_col[:, g, j : j + 1],
                    op0=ALU.max,
                    op1=ALU.mult,
                )

        def turn_and_store(u):
            g, site0, sites = UNITS[u]
            banks = []
            for s in range(sites // P):
                bank = psum.tile([P, SLOTS, P], F32, name="turned")
                for j in range(SLOTS):
                    nc.tensor.transpose(bank[:, j, :], y_rows[u][:, j, P * s : P * (s + 1)], ident[:])
                banks.append(bank)
            for pair in range(sites // (2 * P)):
                y_out = work.tile([P, 2, GROUP], F32, name="y_out", bufs=Y_OUT_BUFS, align_bytes=ALIGN)
                for s in range(2):
                    nc.scalar.copy(
                        out=y_out[:, s, :].rearrange("p (m j) -> p m j", j=SLOTS),
                        in_=banks[2 * pair + s][:].rearrange("p j m -> p m j"),
                    )
                rows = out_0[site0 + 2 * P * pair : site0 + 2 * P * (pair + 1), GROUP * g : GROUP * (g + 1)]
                nc.sync.dma_start(out=rows.rearrange("(s p) n -> p s n", p=P), in_=y_out[:])

        def group_y(u):
            group_rows(("y", u), y_rows[u], UNITS[u][2])

        y_code = {}

        def quantise_y(u):
            g, site0, sites = UNITS[u]
            y_code[u] = work.tile([P, sites], I32, name="y_code", bufs=Y_CODE_BUFS, align_bytes=ALIGN)
            scales = y_scale_early[:, g, :] if g < N_GROUPS - 1 else y_scale_last[:, 0, :]
            quantise(("y", u), y_code[u][:], scales[:, site0 : site0 + sites], sites)

        def store_codes(u):
            g, site0, sites = UNITS[u]
            dst = out_1[g].rearrange("p m j -> p (m j)")[:, SLOTS * site0 : SLOTS * (site0 + sites)]
            nc.sync.dma_start(out=dst.bitcast(I32), in_=y_code[u][:])

        def store_scales(src, g0, g1):
            for r in range(4):
                nc.sync.dma_start(
                    out=out_2[g0:g1, r:16:4, :].rearrange("g q n -> q g n").bitcast(I32),
                    in_=src[r:P:32, :, :].bitcast(I32),
                )


        group_recipe(0, 0)
        order_w_codes(0)
        order_w_scales(0)
        quantise_recipe(0, 0)
        order_w_scales(1)
        order_w_codes(1)
        order_w_scales(2)
        group_recipe(0, 1)
        order_w_codes(2)
        stage1(0)
        group_h(0)
        quantise_recipe(0, 1)
        group_recipe(0, 2)
        quantise_h(0)
        stage1(1)
        group_h(1)
        quantise_recipe(0, 2)
        for i in range(2, H_PIECES):
            stage1(i)
            group_h(i)
            quantise_h(i - 1)

        group_recipe(1, 0, nc.scalar.copy, 0, SLOTS // 2)
        stage2(0, 0)
        finish(0, 0, 1)
        quantise_h(H_PIECES - 1)
        group_recipe(1, 1)
        stage2(0, 1)
        group_recipe(1, 0, nc.scalar.copy, SLOTS // 2, SLOTS)
        quantise_recipe(1, 0)
        group_recipe(1, 2)
        quantise_recipe(1, 1)
        stage2(0, 2)
        stage2(0, 3)
        finish(0, 1, SLOTS)
        quantise_recipe(1, 2)
        group_recipe(2, 0)

        def vector_work(u):
            if u == 1:
                finish(1)
                quantise_recipe(2, 0)
                group_recipe(2, 1)
            elif u == 2:
                finish(2, 0, 2)
                quantise_recipe(2, 1)
                group_recipe(2, 2)
                finish(2, 2, SLOTS)
                quantise_recipe(2, 2)
                group_recipe(3, 0)
            elif u == 3:
                finish(3, 0, 2)
                quantise_recipe(3, 0)
                group_recipe(3, 1)
                finish(3, 2, SLOTS)
                quantise_recipe(3, 1)
                group_recipe(3, 2)
                group_y(0)
                quantise_recipe(3, 2)
            elif u in (4, 5):
                behind = 2 * (u - 4)
                finish(u)
                quantise_y(behind)
                group_y(behind + 1)
                group_y(behind + 2)
                quantise_y(behind + 1)
            else:
                finish(u)
                quantise_y(u - 2)
                group_y(u - 1)

        codes_to_store = {5: [0], 6: [1, 2], 7: [3, 4], 8: [5]}
        for u in range(1, LAST + 1):
            for j in range(SLOTS):
                stage2(u, j)
            for v in codes_to_store.get(u, []):
                store_codes(v)
            if u == LAST:
                store_scales(y_scale_early, 0, N_GROUPS - 1)
            vector_work(u)
            turn_and_store(u - 1)
        store_codes(LAST - 2)
        turn_and_store(LAST)
        group_y(LAST)
        quantise_y(LAST - 1)
        quantise_y(LAST)
        store_codes(LAST - 1)
        store_codes(LAST)
        store_scales(y_scale_last, N_GROUPS - 1, N_GROUPS)
